import numpy as np, ml_dtypes
CORES = [66,74,82,90,194,202,210,218]
N = 8
import mx_ref
BF = ml_dtypes.bfloat16
def entries(a):
    return np.ascontiguousarray(a.T).reshape(-1)
def table(e):
    return np.ascontiguousarray(np.reshape(e, (-1, 16)).T).astype(np.int32)
def f(rng, *shape):
    return mx_ref.flush((rng.standard_normal(shape, dtype=np.float32) * np.exp2(rng.integers(-2, 3, shape[:-1] + (1,)))).astype(BF))
def wide(rng, *shape, cols=0):
    v = rng.standard_normal(shape, dtype=np.float32) * np.exp2(rng.integers(-12, 13, shape)).astype(np.float32)
    if cols: v *= np.repeat(np.exp2(rng.integers(-cols, cols + 1, shape[:-2] + (1, shape[-1] // 4))) * (rng.random(shape[:-2] + (1, shape[-1] // 4)) > 0.0625), 4, axis=-1).astype(np.float32)
    return mx_ref.flush(v.astype(BF))
T, CAPP, OC, UN = 192, 24, 88, 48
HOST = [0 if c < 128 else 1 for c in CORES]
def term(a, B):
    return np.stack([mx_ref.matmul(mx_ref.quantize(a[:, 512 * i:512 * i + 512]), B) for i in range(4)], axis=2).reshape(128, -1)
def padded(e, k):
    return table(np.concatenate([e, np.full(k - len(e), -1)]))
def lists(rng, fixed=False, blocks=False, plain=False, short=False):
    own = [[[] for d in range(N)] for r in range(N)]
    union = np.full((N, 2, UN), -1)
    for d in range(N):
        half = np.arange(OC) if blocks else rng.permutation(OC)
        ext = [rng.choice(half[(1 - g) * (OC // 2):(2 - g) * (OC // 2)], UN - OC // 2, replace=False) for g in range(2)]
        low = int(rng.integers(0, 2)) if short else -1
        for g in range(2):
            R = [r for r in range(N) if HOST[r] == g]
            mine = list(half[g * (OC // 2):(g + 1) * (OC // 2)]) + list(ext[g])
            p = rng.permutation(len(R)); named = [set() for _ in mine]
            for k in range(CAPP):
                if not fixed: p = rng.permutation(len(R))
                for i in range(len(R) // 2): named[k * (len(R) // 2) + i] = {R[p[2 * i]], R[p[2 * i + 1]]}
            if g == low:
                both = [j for j in range(UN) if j >= OC // 2 or mine[j] in ext[1 - g]]
                for j in both:
                    for r in list(named[j]):
                        to = [t for t in range(OC // 2) if t not in both and r not in named[t]]
                        named[j].remove(r); named[rng.choice(to)].add(r)
            elif not (plain or fixed or short):
                for j in range(OC // 2, UN):
                    for r in list(rng.permutation(list(named[j])))[:rng.integers(0, 3)]:
                        to = [t for t in range(OC // 2) if r not in named[t]]
                        named[j].remove(r); named[rng.choice(to)].add(r)
            at = rng.permutation(UN)
            for j, s in enumerate(named):
                if s: union[d, g, at[j]] = mine[j]
                for r in s: own[r][d].append((mine[j], at[j]))
    send, place, un = [], np.full((N, N, CAPP), -1), []
    for r in range(N):
        send.append(table(rng.permutation(T))); u = []
        for d in range(N):
            o = [own[r][d][i] for i in rng.permutation(CAPP)]
            place[d, r] = [v for v, _ in o]; u += [w for _, w in o]
        un.append(table(u))
    return {"send": np.stack(send), "place": np.stack([table(place[d].reshape(-1)) for d in range(N)]), "un": np.stack(un), "upl": np.stack([padded(union[d].reshape(-1), 96) for d in range(N)])}
def setup_inputs(rng):
    return {"a": f(rng, N, 128, 4 * 512), "b": f(rng, N, 128, 4 * T), **lists(rng)}
def setup_inputs_blocks(rng):
    return {**setup_inputs(rng), **lists(rng, blocks=True, plain=True)}
def setup_inputs_lossless(rng):
    d = setup_inputs(rng)
    a = np.zeros((N, 128, 4 * 128, 4), np.float32)
    for r in range(N):
        k = rng.integers(0, 512, size=4 * 128)
        a[r, k // 4, np.arange(4 * 128), k % 4] = 1.0
    size = 2.0 ** rng.integers(-4, 5, size=(N, OC)); b = rng.integers(-1, 2, size=(N, 128, T, 4)).astype(np.float64)
    for r in range(N):
        s = entries(d["send"][r]).reshape(N, CAPP)
        for o in range(N): b[r][:, s[o]] *= size[o][entries(d["place"][o]).reshape(N, CAPP)[r]][None, :, None]
    d["a"], d["b"] = a.reshape(N, 128, 4 * 512).astype(BF), b.reshape(N, 128, 4 * T).astype(np.float32).astype(BF)
    return d
def setup_inputs_pairs(rng):
    return {**setup_inputs(rng), **lists(rng, fixed=True)}
def setup_inputs_short(rng):
    return {**setup_inputs(rng), **lists(rng, short=True)}
def setup_inputs_spread(rng):
    d = setup_inputs(rng); d["b"] = wide(rng, N, 128, 4 * T); return d
def check_inputs(x):
    b = []
    seen = np.zeros((N, OC), int)
    for r in range(N):
        s, u = entries(x["send"][r]), entries(x["un"][r]).reshape(N, CAPP)
        if sorted(s.tolist()) != list(range(T)): b.append("send")
        if u.min() < 0 or u.max() >= UN: b.append("un")
        for o in range(N):
            p = entries(x["place"][o]).reshape(N, CAPP)[r]
            if p.min() < 0 or p.max() >= OC or len(set(p.tolist())) != CAPP: b.append("place")
            w = entries(x["upl"][o])[:2 * UN].reshape(2, UN)[HOST[r]]
            if (w[u[o]] != p).any(): b.append("upl")
            seen[o][p] += 1
    for o in range(N):
        for g in range(2):
            w = entries(x["upl"][o]); bad = w.min() < -1 or w.max() >= OC or (w[2 * UN:] != -1).any(); w = w[:2 * UN].reshape(2, UN)[g]; w = w[w >= 0]
            if len(set(w.tolist())) != len(w): b.append("upl twice")
    if seen.min() < 2: b.append("a column with fewer than two terms")
    return b
def reference(a, b, send, place, un, upl):
    Z = [term(a[r], mx_ref.quantize(b[r])).reshape(128, T, 4) for r in range(N)]
    y = np.zeros((N, 128, 4 * OC), np.float32)
    for o in range(N):
        parts = []
        for r in range(N):
            t = np.zeros((128, OC, 4), np.float32); t[:, entries(place[o]).reshape(N, CAPP)[r]] = Z[r][:, entries(send[r]).reshape(N, CAPP)[o]]
            parts.append(t.reshape(128, 4 * OC))
        y[o] = mx_ref.total(parts)
    return {"y": y}

@@ -1,0 +1,322 @@
+from concourse.bass import DstId, RemoteDMATransfer
+from concourse.mybir import dt, AluOpType, ActivationFunctionType
+
+N, TCOL, CAPP, OC, UN = 8, 192, 24, 88, 48
+H = 4
+FAR = (H - 1) * UN
+OWN0 = H * UN - 128
+LAND = 512
+
+F32, BF, I32, U16 = "float32", "bfloat16", "int32", "uint16"
+CODE, PLANE = "float8_e4m3fn_x4", "uint8"
+SCRATCH = {
+    "asb": ("sbuf", [128, 2048], BF), "bsb": ("sbuf", [128, 4 * TCOL], BF),
+    "sl": ("sbuf", [128, 12], I32), "ul": ("sbuf", [128, 12], I32), "pl": ("sbuf", [128, 6], I32),
+    "ones": ("sbuf", [128, 516], BF), "cst": ("sbuf", [128, 516], BF),
+    "ipm": ("sbuf", [128, 12], I32), "ek": ("sbuf", [128, 12], I32), "q15": ("sbuf", [128, 12], I32),
+    "ent": ("sbuf", [128, 12], I32), "w1": ("sbuf", [128, 12], I32), "w2": ("sbuf", [128, 12], I32),
+    "dsl": ("sbuf", [128, 12], I32), "x1": ("sbuf", [128, 12], I32), "x2": ("sbuf", [128, 12], I32),
+    "offs": ("sbuf", [128, 48], U16), "offu": ("sbuf", [128, 48], U16),
+    "bgf": ("sbuf", [128, 384], BF), "bgn": ("sbuf", [128, 384], BF),
+    "bpf": ("sbuf", [128, 768], BF), "bpn": ("sbuf", [128, 768], BF),
+    "aq": ("sbuf", [128, 512], CODE), "asc": ("sbuf", [128, 512], PLANE),
+    "bfq": ("sbuf", [128, 192], CODE), "bfs": ("sbuf", [128, 192], PLANE),
+    "bnq": ("sbuf", [128, 192], CODE), "bns": ("sbuf", [128, 192], PLANE),
+    "hf": ("sbuf", [128, 4 * FAR], BF), "hfq": ("sbuf", [128, FAR], CODE), "hfs": ("sbuf", [128, FAR], PLANE),
+    "hn": ("sbuf", [128, 4 * FAR], BF), "hnq": ("sbuf", [128, FAR], CODE), "hns": ("sbuf", [128, FAR], PLANE),
+    "hg": ("sbuf", [128, 512], BF), "hgq": ("sbuf", [128, 128], CODE), "hgs": ("sbuf", [128, 128], PLANE),
+    "kq": ("sbuf", [128, LAND + 7 * UN], CODE), "ks": ("sbuf", [128, LAND + 7 * UN], PLANE),
+    "val": ("sbuf", [128, 96], F32), "inv": ("sbuf", [128, 272], F32),
+    "lt": ("sbuf", [128, 6], I32), "tr": ("sbuf", [128, 6], I32), "tm": ("sbuf", [128, 6], I32),
+    "p2": ("sbuf", [128, 6], I32), "p3": ("sbuf", [128, 6], I32), "po": ("sbuf", [128, 6], U16),
+    "rq": ("sbuf", [128, 2], I32), "tq": ("sbuf", [128, 2], I32),
+    "mk": ("sbuf", [128, 4], F32), "tc": ("sbuf", [128, 2], F32),
+    "s0": ("sbuf", [128, 44], F32), "s1": ("sbuf", [128, 44], F32), "s2": ("sbuf", [128, 44], F32),
+    "s3": ("sbuf", [128, 44], F32), "offi": ("sbuf", [128, 44], U16),
+    "sn": ("sbuf", [128, 200], F32), "sf": ("sbuf", [128, 200], F32),
+    "yn": ("sbuf", [128, 4 * OC], F32), "yo": ("sbuf", [128, 4 * OC], F32),
+}
+for _i in range(4):
+    SCRATCH["pa%d" % _i] = ("psum", [128, 512], F32)
+    SCRATCH["pb%d" % _i] = ("psum", [128, 512], F32)
+
+SEMAPHORES = (["sld", "uld", "pld", "bld", "ald0", "ald1", "yst", "lsend", "ones", "gi", "gcst", "gv", "vq", "veq", "voff",
+               "voffn", "vbq", "vbqn", "vf", "vfn", "vg", "vm", "vhf", "vhn", "vhg", "vinv", "vy",
+               "acg", "acn", "acf", "acfn", "acgg", "acnn", "acm", "ayn", "arrm"]
+              + ["vaq%d" % i for i in range(4)] + ["tf%d" % i for i in range(4)] + ["tfn%d" % i for i in range(4)]
+              + ["tg%d" % i for i in range(4)] + ["tn%d" % i for i in range(4)] + ["tl%d" % i for i in range(4)]
+              + ["arrf%d" % i for i in range(3)] + ["arrn%d" % i for i in range(3)])
+
+
+def slot_of(topo, dst, src):
+    if topo.mates(dst, src):
+        return 0
+    return 1 if topo.same_plane(dst, src) else 2
+
+
+CODE_ENG = {0: (4, 2), 1: (6, 2), 2: (0, 4)}
+PLANE_ENG = {0: (0, 2), 1: (2, 2), 2: (4, 4)}
+
+
+def emask(topo, src, dst, first, count):
+    return sum(1 << e for e in topo.engines(src, dst)[first:first + count])
+
+
+def rank_program(g, core, T, topo):
+    rank = T.rank_of(core)
+    if rank is None:
+        return
+    v, s, te, sy, sem = g.vector, g.scalar, g.tensor, g.sync, T.sem
+    add, mult = AluOpType.add, AluOpType.mult
+    copy = ActivationFunctionType.Copy
+    here = [r for r in range(N) if topo.host(T.cores[r]) == topo.host(core)]
+    there = [r for r in range(N) if topo.host(T.cores[r]) != topo.host(core)]
+    my = here.index(rank)
+    f0, n0 = there[0] * CAPP // 16, here[0] * CAPP // 16
+    peers = [T.cores[here[(my + 1 + j) % H]] for j in range(H - 1)]
+    partner = T.cores[there[my]]
+
+    cnt = [0]
+
+    def ch(ins):
+        ins.then_inc(sem.vq, 1)
+        cnt[0] += 1
+
+    def own():
+        v.wait_ge(sem.vq, cnt[0])
+
+    for k in range(8):
+        q = sy if k < 4 else s
+        q.dma_start(T.sl[16 * k:16 * k + 16, :], T.send[:, :]).then_inc(sem.sld, 16)
+    sy.dma_start(T.bsb[:, :], T.b[:, :]).then_inc(sem.bld, 16)
+    sy.dma_start(T.asb[:, 0:1536], T.a[:, 0:1536]).then_inc(sem.ald0, 16)
+    sy.dma_start(T.asb[:, 1536:2048], T.a[:, 1536:2048]).then_inc(sem.ald1, 16)
+    for k in range(8):
+        s.dma_start(T.ul[16 * k:16 * k + 16, :], T.un[:, :]).then_inc(sem.uld, 16)
+    for k in range(8):
+        sy.dma_start(T.pl[16 * k:16 * k + 16, :], T.upl[:, :]).then_inc(sem.pld, 16)
+
+    g.iota(T.ipm[:, :], [[0, 12]], 0, 1).then_inc(sem.gi, 1)
+    g.iota(T.ek[:, :], [[16, 12]], 0, 0).then_inc(sem.gi, 1)
+    g.wait_ge(sem.ones, 1)
+    g.affine_select(T.cst[:, :], T.ones[:, :], [[1, 516]], AluOpType.is_equal, 0.0, -3, -4).then_inc(sem.gcst, 1)
+    g.iota(T.val[:, :], [[0, 2], [1, 48]], 0, 0, allow_small_or_imprecise_dtypes=True).then_inc(sem.gv, 1)
+
+    v.memset(T.ones[:, :], 1.0).then_inc(sem.ones, 1)
+    ch(v.memset(T.bpf[:, :], 0.0))
+    v.wait_ge(sem.gi, 2)
+    ch(v.tensor_scalar(T.q15[:, :], T.ipm[:, :], 15, None, AluOpType.bitwise_and))
+    own()
+    ch(v.tensor_tensor(T.ent[:, :], T.q15[:, :], T.ek[:, :], add))
+    own()
+    ch(v.tensor_scalar(T.w1[:, :], T.ent[:, :], 683, (3 - my) << 14, mult, add))
+    own()
+    ch(v.tensor_scalar(T.w2[:, :], T.w1[:, :], 14, 3, AluOpType.arith_shift_right, AluOpType.bitwise_and))
+    own()
+    ch(v.tensor_scalar(T.dsl[:, :], T.w2[:, :], 4 * UN, None, mult))
+    ch(v.memset(T.bpn[:, :], 0.0))
+    ch(v.memset(T.hg[:, :], 0.0))
+    ch(v.memset(T.sn[:, 192:200], 0.0))
+    ch(v.memset(T.sf[:, 192:200], 0.0))
+    ch(v.memset(T.inv[:, :], float(UN)))
+    v.wait_ge(sem.gcst, 1)
+    for t in range(4):
+        v.quantize_mx(T.kq[:, 128 * t:128 * t + 128], T.ks[:, 128 * t:128 * t + 128],
+                      T.cst[:, 3 - t:515 - t]).then_inc(sem.veq, 1)
+
+    v.wait_ge(sem.sld, 128)
+    for t in range(4):
+        v.tensor_scalar(T.offs[:, 6 * t:6 * t + 6], T.sl[:, f0:f0 + 6], 4, t, mult, add).then_inc(sem.voff, 1)
+    v.wait_ge(sem.uld, 128)
+    ch(v.tensor_scalar(T.x1[:, :], T.ul[:, :], 4, None, mult))
+    own()
+    ch(v.tensor_tensor(T.x2[:, :], T.x1[:, :], T.dsl[:, :], add))
+    own()
+    for t in range(4):
+        ch(v.tensor_scalar(T.offu[:, 6 * t:6 * t + 6], T.x2[:, f0:f0 + 6], t, None, add))
+    for q in (v, s):
+        q.wait_ge(sem.bld, 16)
+        q.wait_ge(sem.voff, 4)
+    ch(v.tensor_copy(T.bgf[:, 0:192], T.bsb[:, 0:768].indirect(T.offs[:, 0:12])))
+    s.activation(T.bgf[:, 192:384], T.bsb[:, 0:768].indirect(T.offs[:, 12:24]), copy).then_inc(sem.acg, 1)
+    v.wait_ge(sem.acg, 1)
+    own()
+    ch(v.tensor_copy(T.bpf[:, 0:768].indirect(T.offu[:, 0:24]), T.bgf[:, :]))
+    own()
+    v.quantize_mx(T.bfq[:, :], T.bfs[:, :], T.bpf[:, :]).then_inc(sem.vbq, 1)
+    for t in range(4):
+        v.tensor_scalar(T.offs[:, 24 + 6 * t:30 + 6 * t], T.sl[:, n0:n0 + 6], 4, t, mult, add).then_inc(sem.voffn, 1)
+    for t in range(4):
+        ch(v.tensor_scalar(T.offu[:, 24 + 6 * t:30 + 6 * t], T.x2[:, n0:n0 + 6], t, None, add))
+    s.wait_ge(sem.voffn, 4)
+    s.activation(T.bgn[:, :], T.bsb[:, 0:768].indirect(T.offs[:, 24:48]), copy).then_inc(sem.acn, 1)
+
+    for i in range(4):
+        if i == 0:
+            v.wait_ge(sem.ald0, 16)
+        if i == 3:
+            v.wait_ge(sem.ald1, 16)
+        v.quantize_mx(T.aq[:, 128 * i:128 * i + 128], T.asc[:, 128 * i:128 * i + 128],
+                      T.asb[:, 512 * i:512 * i + 512]).then_inc(sem["vaq%d" % i], 1)
+    te.wait_ge(sem.vbq, 1)
+
+    def product(bank, i, q, p, c0, c1, start, stop):
+        return te.matmul_mx(T[bank + str(i)][:, 0:c1 - c0], T.aq[:, 128 * i:128 * i + 128], T.asc[:, 128 * i:128 * i + 128],
+                            T[q][:, c0:c1], T[p][:, c0:c1], start, stop)
+
+    def unpack(bank, t, end, start, stop):
+        return te.matmul_mx(T[bank + str(t)][:, 0:128], T.kq[:, 128 * t:128 * t + 128], T.ks[:, 128 * t:128 * t + 128],
+                            T.kq[:, end - 128:end], T.ks[:, end - 128:end], start, stop)
+
+    for i in range(4):
+        te.wait_ge(sem["vaq%d" % i], 1)
+        product("pa", i, "bfq", "bfs", 0, FAR, True, True).then_inc(sem["tf%d" % i], 1)
+    for i in range(4):
+        product("pb", i, "bfq", "bfs", OWN0, H * UN, True, False)
+    for i in range(3):
+        s.wait_ge(sem["tf%d" % i], 1)
+        s.activation(T.hf[:, i:4 * FAR:4], T["pa%d" % i][:, 0:FAR], copy).then_inc(sem.acf, 1)
+    v.wait_ge(sem.tf3, 1)
+    v.tensor_copy(T.hf[:, 3:4 * FAR:4], T.pa3[:, 0:FAR]).then_inc(sem.vf, 1)
+    v.wait_ge(sem.vf, 1)
+    v.wait_ge(sem.acf, 3)
+    v.quantize_mx(T.hfq[:, :], T.hfs[:, :], T.hf[:, :]).then_inc(sem.vhf, 1)
+
+    def spread(q, p, at, name):
+        codes, planes = [], []
+        for j, d in enumerate(peers):
+            k = slot_of(topo, d, core)
+            rid, pid = topo.addr(d, core)
+            a, b = at + UN * k, at + UN * (k + 1)
+            codes.append(RemoteDMATransfer(
+                dst_ids=[DstId(rid=rid, pnc=pid)], dma_engine_mask=emask(topo, core, d, *CODE_ENG[k]),
+                remote_sem=sem[name + str(k)], src=T[q][:, UN * j:UN * j + UN].bitcast(dt.uint8),
+                dst=T.kq[:, a:b].bitcast(dt.uint8)))
+            planes.append(RemoteDMATransfer(
+                dst_ids=[DstId(rid=rid, pnc=pid)], dma_engine_mask=emask(topo, core, d, *PLANE_ENG[k]),
+                remote_sem=sem[name + str(k)], src=T[p][:, UN * j:UN * j + UN], dst=T.ks[:, a:b]))
+        g.remote_dma_fused(codes, local_sem=sem.lsend)
+        g.remote_dma_fused(planes, local_sem=sem.lsend)
+
+    g.wait_ge(sem.vhf, 1)
+    spread("hfq", "hfs", LAND, "arrf")
+
+    v.wait_ge(sem.acn, 1)
+    own()
+    ch(v.tensor_copy(T.bpn[:, 0:768].indirect(T.offu[:, 24:48]), T.bgn[:, :]))
+    own()
+    v.quantize_mx(T.bnq[:, :], T.bns[:, :], T.bpn[:, :]).then_inc(sem.vbqn, 1)
+    te.wait_ge(sem.vbqn, 1)
+    te.wait_ge(sem.acf, 3)
+    te.wait_ge(sem.vf, 1)
+    for i in range(4):
+        product("pa", i, "bnq", "bns", 0, FAR, True, True).then_inc(sem["tfn%d" % i], 1)
+    for i in range(4):
+        if i % 2 == 0:
+            s.wait_ge(sem["tfn%d" % i], 1)
+            s.activation(T.hn[:, i:4 * FAR:4], T["pa%d" % i][:, 0:FAR], copy).then_inc(sem.acfn, 1)
+        else:
+            v.wait_ge(sem["tfn%d" % i], 1)
+            v.tensor_copy(T.hn[:, i:4 * FAR:4], T["pa%d" % i][:, 0:FAR]).then_inc(sem.vfn, 1)
+    v.wait_ge(sem.acfn, 2)
+    v.wait_ge(sem.vfn, 2)
+    v.quantize_mx(T.hnq[:, :], T.hns[:, :], T.hn[:, :]).then_inc(sem.vhn, 1)
+    g.wait_ge(sem.vhn, 1)
+    spread("hnq", "hns", LAND + 3 * UN, "arrn")
+
+    te.wait_ge(sem.veq, 4)
+    for k in range(3):
+        te.wait_ge(sem["arrf%d" % k], CODE_ENG[k][1] + PLANE_ENG[k][1])
+        for t in range(4):
+            m = unpack("pb", t, LAND + UN * (k + 1), False, k == 2)
+            if k == 2:
+                m.then_inc(sem["tg%d" % t], 1)
+    for t in range(4):
+        if t % 2 == 0:
+            s.wait_ge(sem["tg%d" % t], 1)
+            s.activation(T.hg[:, 320 + t:512:4], T["pb%d" % t][:, 80:128], copy).then_inc(sem.acgg, 1)
+        else:
+            v.wait_ge(sem["tg%d" % t], 1)
+            v.tensor_copy(T.hg[:, 320 + t:512:4], T["pb%d" % t][:, 80:128]).then_inc(sem.vg, 1)
+    v.wait_ge(sem.acgg, 2)
+    v.wait_ge(sem.vg, 2)
+    v.quantize_mx(T.hgq[:, :], T.hgs[:, :], T.hg[:, :]).then_inc(sem.vhg, 1)
+    rid, pid = topo.addr(partner, core)
+    m8 = emask(topo, core, partner, 0, 8)
+    at = LAND + 6 * UN
+    g.wait_ge(sem.vhg, 1)
+    g.remote_dma(T.kq[:, at:at + UN].bitcast(dt.uint8), T.hgq[:, 80:128].bitcast(dt.uint8), sem.arrm, sem.lsend, pid, rid, m8)
+    g.remote_dma(T.ks[:, at:at + UN], T.hgs[:, 80:128], sem.arrm, sem.lsend, pid, rid, m8)
+
+    te.wait_ge(sem.acfn, 2)
+    te.wait_ge(sem.vfn, 2)
+    for i in range(4):
+        product("pa", i, "bnq", "bns", OWN0, H * UN, True, False)
+    for k in range(3):
+        te.wait_ge(sem["arrn%d" % k], CODE_ENG[k][1] + PLANE_ENG[k][1])
+        for t in range(4):
+            m = unpack("pa", t, LAND + UN * (4 + k), False, k == 2)
+            if k == 2:
+                m.then_inc(sem["tn%d" % t], 1)
+    for t in range(4):
+        s.wait_ge(sem["tn%d" % t], 1)
+        s.activation(T.sn[:, t:192:4], T["pa%d" % t][:, 80:128], copy).then_inc(sem.acnn, 1)
+
+    v.wait_ge(sem.pld, 128)
+    ch(v.tensor_scalar(T.lt[:, :], T.pl[:, :], 0, None, AluOpType.is_lt))
+    ch(v.tensor_scalar(T.tr[:, 0:3], T.ent[:, 0:3], 2 * OC + 1, None, add))
+    ch(v.tensor_scalar(T.tr[:, 3:6], T.ent[:, 3:6], OC + 1, None, add))
+    ch(v.tensor_scalar(T.p2[:, 0:3], T.pl[:, 0:3], 0, None, add))
+    ch(v.tensor_scalar(T.p2[:, 3:6], T.pl[:, 3:6], OC, None, add))
+    ch(v.tensor_scalar(T.rq[:, :], T.ipm[:, 0:2], 2, 3, AluOpType.arith_shift_right, AluOpType.bitwise_and))
+    ch(v.tensor_scalar(T.tq[:, :], T.ipm[:, 0:2], 3, None, AluOpType.bitwise_and))
+    own()
+    ch(v.tensor_tensor(T.tm[:, :], T.lt[:, :], T.tr[:, :], mult))
+    for r in range(4):
+        ch(v.tensor_scalar(T.mk[:, r:r + 1], T.rq[:, 0:1], r, 4, AluOpType.is_equal, mult))
+    ch(v.tensor_copy(T.tc[:, :], T.tq[:, :]))
+    own()
+    ch(v.tensor_tensor(T.p3[:, :], T.p2[:, :], T.tm[:, :], add))
+    own()
+    ch(v.tensor_copy(T.po[:, :], T.p3[:, :]))
+    v.wait_ge(sem.gv, 1)
+    own()
+    ch(v.tensor_copy(T.inv[:, 0:272].indirect(T.po[:, 0:6]), T.val[:, :]))
+    own()
+    ch(v.tensor_scalar(T.s0[:, :], T.inv[:, 0:176:4], T.mk[:, 0:1], T.tc[:, 0:1], mult, add))
+    for r in range(1, 4):
+        ch(v.tensor_scalar(T["s%d" % r][:, :], T.inv[:, r:176:4], T.mk[:, r:r + 1], None, mult))
+    own()
+    ch(v.tensor_tensor(T.s0[:, :], T.s0[:, :], T.s1[:, :], add))
+    ch(v.tensor_tensor(T.s2[:, :], T.s2[:, :], T.s3[:, :], add))
+    own()
+    ch(v.tensor_tensor(T.s0[:, :], T.s0[:, :], T.s2[:, :], add))
+    own()
+    v.tensor_copy(T.offi[:, :], T.s0[:, :]).then_inc(sem.vinv, 1)
+    gn, gf = 22 * topo.host(core), 22 * topo.host(partner)
+    s.wait_ge(sem.vinv, 1)
+    s.wait_ge(sem.acnn, 4)
+    s.activation(T.yn[:, :], T.sn[:, 0:200].indirect(T.offi[:, gn:gn + 22]), copy).then_inc(sem.ayn, 1)
+
+    te.wait_ge(sem.arrm, 16)
+    te.wait_ge(sem.acgg, 2)
+    te.wait_ge(sem.vg, 2)
+    for t in range(4):
+        unpack("pb", t, at + UN, True, True).then_inc(sem["tl%d" % t], 1)
+    for t in range(4):
+        if t % 2 == 0:
+            s.wait_ge(sem["tl%d" % t], 1)
+            s.activation(T.sf[:, t:192:4], T["pb%d" % t][:, 80:128], copy).then_inc(sem.acm, 1)
+        else:
+            v.wait_ge(sem["tl%d" % t], 1)
+            v.tensor_copy(T.sf[:, t:192:4], T["pb%d" % t][:, 80:128]).then_inc(sem.vm, 1)
+    own()
+    v.wait_ge(sem.vinv, 1)
+    v.wait_ge(sem.ayn, 1)
+    v.wait_ge(sem.acm, 2)
+    v.wait_ge(sem.vm, 2)
+    v.tensor_tensor(T.yo[:, :], T.sf[:, 0:200].indirect(T.offi[:, gf:gf + 22]), T.yn[:, :], add).then_inc(sem.vy, 1)
+    sy.wait_ge(sem.vy, 1)
+    sy.dma_start(T.y[:, :], T.yo[:, :]).then_inc(sem.yst, 16)
+    sy.wait_ge(sem.yst, 16)
+    g.wait_ge(sem.lsend, 48)

@@ -4,8 +4,9 @@ from concourse.mybir import dt, AluOpType, ActivationFunctionType
 N, TCOL, CAPP, OC, UN = 8, 192, 24, 88, 48
 H = 4
 FAR = (H - 1) * UN
-OWN0 = H * UN - 128
 LAND = 512
+OP = 96
+WIN = 56
 
 F32, BF, I32, U16 = "float32", "bfloat16", "int32", "uint16"
 CODE, PLANE = "float8_e4m3fn_x4", "uint8"
@@ -15,36 +16,37 @@ SCRATCH = {
     "ones": ("sbuf", [128, 516], BF), "cst": ("sbuf", [128, 516], BF),
     "ipm": ("sbuf", [128, 12], I32), "ek": ("sbuf", [128, 12], I32), "q15": ("sbuf", [128, 12], I32),
     "ent": ("sbuf", [128, 12], I32), "w1": ("sbuf", [128, 12], I32), "w2": ("sbuf", [128, 12], I32),
-    "dsl": ("sbuf", [128, 12], I32), "x1": ("sbuf", [128, 12], I32), "x2": ("sbuf", [128, 12], I32),
+    "dsl": ("sbuf", [128, 12], I32), "x2": ("sbuf", [128, 12], I32),
     "offs": ("sbuf", [128, 48], U16), "offu": ("sbuf", [128, 48], U16),
     "bgf": ("sbuf", [128, 384], BF), "bgn": ("sbuf", [128, 384], BF),
-    "bpf": ("sbuf", [128, 768], BF), "bpn": ("sbuf", [128, 768], BF),
+    "bpf": ("sbuf", [128, 8 * FAR], BF), "bpn": ("sbuf", [128, 8 * FAR], BF),
     "aq": ("sbuf", [128, 512], CODE), "asc": ("sbuf", [128, 512], PLANE),
-    "bfq": ("sbuf", [128, 192], CODE), "bfs": ("sbuf", [128, 192], PLANE),
-    "bnq": ("sbuf", [128, 192], CODE), "bns": ("sbuf", [128, 192], PLANE),
+    "bfq": ("sbuf", [128, 2 * FAR], CODE), "bfs": ("sbuf", [128, 2 * FAR], PLANE),
+    "bnq": ("sbuf", [128, 2 * FAR], CODE), "bns": ("sbuf", [128, 2 * FAR], PLANE),
     "hf": ("sbuf", [128, 4 * FAR], BF), "hfq": ("sbuf", [128, FAR], CODE), "hfs": ("sbuf", [128, FAR], PLANE),
     "hn": ("sbuf", [128, 4 * FAR], BF), "hnq": ("sbuf", [128, FAR], CODE), "hns": ("sbuf", [128, FAR], PLANE),
     "hg": ("sbuf", [128, 512], BF), "hgq": ("sbuf", [128, 128], CODE), "hgs": ("sbuf", [128, 128], PLANE),
     "kq": ("sbuf", [128, LAND + 7 * UN], CODE), "ks": ("sbuf", [128, LAND + 7 * UN], PLANE),
-    "val": ("sbuf", [128, 96], F32), "inv": ("sbuf", [128, 272], F32),
+    "mg": ("sbuf", [128, 4 * UN], F32), "xg": ("sbuf", [128, 4 * UN], F32),
+    "mn": ("sbuf", [128, 4 * UN], F32), "xn": ("sbuf", [128, 4 * UN], F32),
+    "val": ("sbuf", [128, 96], F32), "inv": ("sbuf", [128, 288], F32), "rv": ("sbuf", [128, 192], F32),
+    "m16": ("sbuf", [128, 192], F32), "pf": ("sbuf", [128, 2], F32),
     "lt": ("sbuf", [128, 6], I32), "tr": ("sbuf", [128, 6], I32), "tm": ("sbuf", [128, 6], I32),
-    "p2": ("sbuf", [128, 6], I32), "p3": ("sbuf", [128, 6], I32), "po": ("sbuf", [128, 6], U16),
-    "rq": ("sbuf", [128, 2], I32), "tq": ("sbuf", [128, 2], I32),
-    "mk": ("sbuf", [128, 4], F32), "tc": ("sbuf", [128, 2], F32),
-    "s0": ("sbuf", [128, 44], F32), "s1": ("sbuf", [128, 44], F32), "s2": ("sbuf", [128, 44], F32),
-    "s3": ("sbuf", [128, 44], F32), "offi": ("sbuf", [128, 44], U16),
-    "sn": ("sbuf", [128, 200], F32), "sf": ("sbuf", [128, 200], F32),
-    "yn": ("sbuf", [128, 4 * OC], F32), "yo": ("sbuf", [128, 4 * OC], F32),
+    "p1": ("sbuf", [128, 6], I32), "p2": ("sbuf", [128, 6], I32), "p3": ("sbuf", [128, 6], I32),
+    "p4": ("sbuf", [128, 6], I32), "p5": ("sbuf", [128, 6], I32), "po": ("sbuf", [128, 6], U16),
+    "f0": ("sbuf", [128, 192], F32), "f1": ("sbuf", [128, 96], F32), "f2": ("sbuf", [128, 48], F32),
+    "f3": ("sbuf", [128, 24], F32), "f4": ("sbuf", [128, 12], F32), "offi": ("sbuf", [128, 12], U16),
+    "sn": ("sbuf", [128, 4 * WIN], F32), "sf": ("sbuf", [128, 4 * WIN], F32),
+    "yn": ("sbuf", [128, 4 * OP], F32), "yo": ("sbuf", [128, 4 * OP], F32),
 }
 for _i in range(4):
     SCRATCH["pa%d" % _i] = ("psum", [128, 512], F32)
     SCRATCH["pb%d" % _i] = ("psum", [128, 512], F32)
 
-SEMAPHORES = (["sld", "uld", "pld", "bld", "ald0", "ald1", "yst", "lsend", "ones", "gi", "gcst", "gv", "vq", "veq", "voff",
-               "voffn", "vbq", "vbqn", "vf", "vfn", "vg", "vm", "vhf", "vhn", "vhg", "vinv", "vy",
-               "acg", "acn", "acf", "acfn", "acgg", "acnn", "acm", "ayn", "arrm"]
-              + ["vaq%d" % i for i in range(4)] + ["tf%d" % i for i in range(4)] + ["tfn%d" % i for i in range(4)]
-              + ["tg%d" % i for i in range(4)] + ["tn%d" % i for i in range(4)] + ["tl%d" % i for i in range(4)]
+SEMAPHORES = (["sld", "uld", "pld", "bld", "ald0", "ald1", "yst", "lsend", "ones", "gi", "gcst", "gz", "gh", "gv", "gr", "vc",
+               "vq", "vi", "vz", "veq", "voff", "voffn", "vbq", "vbqn", "vbo", "vbno", "vf", "vg", "vhf", "vhn",
+               "vhg", "vinv", "vy", "acg", "acn", "acf", "acfn", "ayn", "arrm"]
+              + [p + str(i) for p in ("vaq", "tf", "tfn", "tg", "tn", "tl", "ag", "an", "am", "vx", "vn") for i in range(4)]
               + ["arrf%d" % i for i in range(3)] + ["arrn%d" % i for i in range(3)])
 
 
@@ -76,23 +78,25 @@ def rank_program(g, core, T, topo):
     peers = [T.cores[here[(my + 1 + j) % H]] for j in range(H - 1)]
     partner = T.cores[there[my]]
 
-    cnt = [0]
+    cnt = {"vc": 0, "vq": 0, "vi": 0, "vz": 0, "vx0": 0, "vx1": 0, "vx2": 0, "vx3": 0}
 
-    def ch(ins):
-        ins.then_inc(sem.vq, 1)
-        cnt[0] += 1
+    def ch(name, ins):
+        ins.then_inc(sem[name], 1)
+        cnt[name] += 1
 
-    def own():
-        v.wait_ge(sem.vq, cnt[0])
+    def own(name):
+        v.wait_ge(sem[name], cnt[name])
+
+    def fill(out, pattern, base, done):
+        g.iota(out, pattern, base, 0, allow_small_or_imprecise_dtypes=True).then_inc(done, 1)
 
     for k in range(8):
-        q = sy if k < 4 else s
-        q.dma_start(T.sl[16 * k:16 * k + 16, :], T.send[:, :]).then_inc(sem.sld, 16)
+        (sy if k < 4 else s).dma_start(T.sl[16 * k:16 * k + 16, :], T.send[:, :]).then_inc(sem.sld, 16)
     sy.dma_start(T.bsb[:, :], T.b[:, :]).then_inc(sem.bld, 16)
+    for k in range(8):
+        (sy if k < 3 else s).dma_start(T.ul[16 * k:16 * k + 16, :], T.un[:, :]).then_inc(sem.uld, 16)
     sy.dma_start(T.asb[:, 0:1536], T.a[:, 0:1536]).then_inc(sem.ald0, 16)
     sy.dma_start(T.asb[:, 1536:2048], T.a[:, 1536:2048]).then_inc(sem.ald1, 16)
-    for k in range(8):
-        s.dma_start(T.ul[16 * k:16 * k + 16, :], T.un[:, :]).then_inc(sem.uld, 16)
     for k in range(8):
         sy.dma_start(T.pl[16 * k:16 * k + 16, :], T.upl[:, :]).then_inc(sem.pld, 16)
 
@@ -100,86 +104,79 @@ def rank_program(g, core, T, topo):
     g.iota(T.ek[:, :], [[16, 12]], 0, 0).then_inc(sem.gi, 1)
     g.wait_ge(sem.ones, 1)
     g.affine_select(T.cst[:, :], T.ones[:, :], [[1, 516]], AluOpType.is_equal, 0.0, -3, -4).then_inc(sem.gcst, 1)
-    g.iota(T.val[:, :], [[0, 2], [1, 48]], 0, 0, allow_small_or_imprecise_dtypes=True).then_inc(sem.gv, 1)
+    fill(T.bpn[:, :], [[0, 8 * FAR]], 0, sem.gz)
+    fill(T.rv[:, :], [[1, 16], [0, 12]], 0, sem.gr)
 
     v.memset(T.ones[:, :], 1.0).then_inc(sem.ones, 1)
-    ch(v.memset(T.bpf[:, :], 0.0))
     v.wait_ge(sem.gi, 2)
-    ch(v.tensor_scalar(T.q15[:, :], T.ipm[:, :], 15, None, AluOpType.bitwise_and))
-    own()
-    ch(v.tensor_tensor(T.ent[:, :], T.q15[:, :], T.ek[:, :], add))
-    own()
-    ch(v.tensor_scalar(T.w1[:, :], T.ent[:, :], 683, (3 - my) << 14, mult, add))
-    own()
-    ch(v.tensor_scalar(T.w2[:, :], T.w1[:, :], 14, 3, AluOpType.arith_shift_right, AluOpType.bitwise_and))
-    own()
-    ch(v.tensor_scalar(T.dsl[:, :], T.w2[:, :], 4 * UN, None, mult))
-    ch(v.memset(T.bpn[:, :], 0.0))
-    ch(v.memset(T.hg[:, :], 0.0))
-    ch(v.memset(T.sn[:, 192:200], 0.0))
-    ch(v.memset(T.sf[:, 192:200], 0.0))
-    ch(v.memset(T.inv[:, :], float(UN)))
-    v.wait_ge(sem.gcst, 1)
-    for t in range(4):
-        v.quantize_mx(T.kq[:, 128 * t:128 * t + 128], T.ks[:, 128 * t:128 * t + 128],
-                      T.cst[:, 3 - t:515 - t]).then_inc(sem.veq, 1)
+    ch("vc", v.tensor_scalar(T.q15[:, :], T.ipm[:, :], 15, None, AluOpType.bitwise_and))
+    ch("vq", v.memset(T.bpf[:, 0:768], 0.0))
+    own("vc")
+    ch("vc", v.tensor_tensor(T.ent[:, :], T.q15[:, :], T.ek[:, :], add))
+    ch("vi", v.tensor_copy(T.pf[:, :], T.q15[:, 0:2]))
+    own("vc")
+    ch("vc", v.tensor_scalar(T.w1[:, :], T.ent[:, :], 683, (3 - my) << 14, mult, add))
+    ch("vi", v.tensor_scalar(T.tr[:, 0:3], T.ent[:, 0:3], 13, None, add))
+    ch("vi", v.tensor_scalar(T.tr[:, 3:6], T.ent[:, 3:6], 7, None, add))
+    own("vc")
+    ch("vc", v.tensor_scalar(T.w2[:, :], T.w1[:, :], 14, 3, AluOpType.arith_shift_right, AluOpType.bitwise_and))
+    own("vc")
+    ch("vc", v.tensor_scalar(T.dsl[:, :], T.w2[:, :], UN, None, mult))
 
     v.wait_ge(sem.sld, 128)
     for t in range(4):
         v.tensor_scalar(T.offs[:, 6 * t:6 * t + 6], T.sl[:, f0:f0 + 6], 4, t, mult, add).then_inc(sem.voff, 1)
     v.wait_ge(sem.uld, 128)
-    ch(v.tensor_scalar(T.x1[:, :], T.ul[:, :], 4, None, mult))
-    own()
-    ch(v.tensor_tensor(T.x2[:, :], T.x1[:, :], T.dsl[:, :], add))
-    own()
-    for t in range(4):
-        ch(v.tensor_scalar(T.offu[:, 6 * t:6 * t + 6], T.x2[:, f0:f0 + 6], t, None, add))
-    for q in (v, s):
-        q.wait_ge(sem.bld, 16)
-        q.wait_ge(sem.voff, 4)
-    ch(v.tensor_copy(T.bgf[:, 0:192], T.bsb[:, 0:768].indirect(T.offs[:, 0:12])))
-    s.activation(T.bgf[:, 192:384], T.bsb[:, 0:768].indirect(T.offs[:, 12:24]), copy).then_inc(sem.acg, 1)
-    v.wait_ge(sem.acg, 1)
-    own()
-    ch(v.tensor_copy(T.bpf[:, 0:768].indirect(T.offu[:, 0:24]), T.bgf[:, :]))
-    own()
-    v.quantize_mx(T.bfq[:, :], T.bfs[:, :], T.bpf[:, :]).then_inc(sem.vbq, 1)
+    own("vc")
+    ch("vc", v.tensor_tensor(T.x2[:, :], T.ul[:, :], T.dsl[:, :], add))
     for t in range(4):
         v.tensor_scalar(T.offs[:, 24 + 6 * t:30 + 6 * t], T.sl[:, n0:n0 + 6], 4, t, mult, add).then_inc(sem.voffn, 1)
+    own("vc")
     for t in range(4):
-        ch(v.tensor_scalar(T.offu[:, 24 + 6 * t:30 + 6 * t], T.x2[:, n0:n0 + 6], t, None, add))
+        ch("vq", v.tensor_scalar(T.offu[:, 6 * t:6 * t + 6], T.x2[:, f0:f0 + 6], 4, t, mult, add))
+    s.wait_ge(sem.bld, 16)
+    s.wait_ge(sem.voff, 4)
+    s.activation(T.bgf[:, :], T.bsb[:, 0:768].indirect(T.offs[:, 0:24]), copy).then_inc(sem.acg, 1)
     s.wait_ge(sem.voffn, 4)
     s.activation(T.bgn[:, :], T.bsb[:, 0:768].indirect(T.offs[:, 24:48]), copy).then_inc(sem.acn, 1)
+    own("vq")
+    v.wait_ge(sem.acg, 1)
+    ch("vq", v.tensor_copy(T.bpf[:, 0:768].indirect(T.offu[:, 0:24]), T.bgf[:, :]))
 
-    for i in range(4):
-        if i == 0:
-            v.wait_ge(sem.ald0, 16)
-        if i == 3:
-            v.wait_ge(sem.ald1, 16)
+    def quantise_a(i):
         v.quantize_mx(T.aq[:, 128 * i:128 * i + 128], T.asc[:, 128 * i:128 * i + 128],
                       T.asb[:, 512 * i:512 * i + 512]).then_inc(sem["vaq%d" % i], 1)
+
+    v.wait_ge(sem.ald0, 16)
+    quantise_a(0)
+    own("vq")
+    v.quantize_mx(T.bfq[:, 0:FAR], T.bfs[:, 0:FAR], T.bpf[:, 0:4 * FAR]).then_inc(sem.vbq, 1)
+    quantise_a(1)
+    quantise_a(2)
+    v.wait_ge(sem.ald1, 16)
+    quantise_a(3)
+    for t in range(4):
+        ch("vq", v.tensor_scalar(T.offu[:, 24 + 6 * t:30 + 6 * t], T.x2[:, n0:n0 + 6], 4, t, mult, add))
+
+    def product(bank, i, q, p, c0, stop):
+        return te.matmul_mx(T[bank + str(i)][:, 0:FAR], T.aq[:, 128 * i:128 * i + 128], T.asc[:, 128 * i:128 * i + 128],
+                            T[q][:, c0:c0 + FAR], T[p][:, c0:c0 + FAR], True, stop)
+
+    def unpack(bank, t, c0, n, start):
+        return te.matmul_mx(T[bank + str(t)][:, 0:n], T.kq[:, 128 * t:128 * t + 128], T.ks[:, 128 * t:128 * t + 128],
+                            T.kq[:, c0:c0 + n], T.ks[:, c0:c0 + n], start, True)
+
     te.wait_ge(sem.vbq, 1)
-
-    def product(bank, i, q, p, c0, c1, start, stop):
-        return te.matmul_mx(T[bank + str(i)][:, 0:c1 - c0], T.aq[:, 128 * i:128 * i + 128], T.asc[:, 128 * i:128 * i + 128],
-                            T[q][:, c0:c1], T[p][:, c0:c1], start, stop)
-
-    def unpack(bank, t, end, start, stop):
-        return te.matmul_mx(T[bank + str(t)][:, 0:128], T.kq[:, 128 * t:128 * t + 128], T.ks[:, 128 * t:128 * t + 128],
-                            T.kq[:, end - 128:end], T.ks[:, end - 128:end], start, stop)
-
     for i in range(4):
         te.wait_ge(sem["vaq%d" % i], 1)
-        product("pa", i, "bfq", "bfs", 0, FAR, True, True).then_inc(sem["tf%d" % i], 1)
-    for i in range(4):
-        product("pb", i, "bfq", "bfs", OWN0, H * UN, True, False)
+        product("pa", i, "bfq", "bfs", 0, True).then_inc(sem["tf%d" % i], 1)
     for i in range(3):
         s.wait_ge(sem["tf%d" % i], 1)
         s.activation(T.hf[:, i:4 * FAR:4], T["pa%d" % i][:, 0:FAR], copy).then_inc(sem.acf, 1)
     v.wait_ge(sem.tf3, 1)
     v.tensor_copy(T.hf[:, 3:4 * FAR:4], T.pa3[:, 0:FAR]).then_inc(sem.vf, 1)
-    v.wait_ge(sem.vf, 1)
     v.wait_ge(sem.acf, 3)
+    v.wait_ge(sem.vf, 1)
     v.quantize_mx(T.hfq[:, :], T.hfs[:, :], T.hf[:, :]).then_inc(sem.vhf, 1)
 
     def spread(q, p, at, name):
@@ -200,46 +197,93 @@ def rank_program(g, core, T, topo):
 
     g.wait_ge(sem.vhf, 1)
     spread("hfq", "hfs", LAND, "arrf")
+    fill(T.inv[:, :], [[0, 288]], UN, sem.gv)
+    fill(T.val[:, :], [[0, 2], [1, 48]], 0, sem.gv)
+    fill(T.hg[:, 0:320], [[0, 320]], 0, sem.gh)
 
     v.wait_ge(sem.acn, 1)
-    own()
-    ch(v.tensor_copy(T.bpn[:, 0:768].indirect(T.offu[:, 24:48]), T.bgn[:, :]))
-    own()
-    v.quantize_mx(T.bnq[:, :], T.bns[:, :], T.bpn[:, :]).then_inc(sem.vbqn, 1)
+    v.wait_ge(sem.gz, 1)
+    own("vq")
+    ch("vq", v.tensor_copy(T.bpn[:, 0:768].indirect(T.offu[:, 24:48]), T.bgn[:, :]))
+    ch("vz", v.memset(T.bpf[:, 768:8 * FAR], 0.0))
+    v.wait_ge(sem.pld, 128)
+    ch("vi", v.tensor_scalar(T.p1[:, :], T.pl[:, :], 15, None, AluOpType.bitwise_and))
+    own("vq")
+    v.quantize_mx(T.bnq[:, 0:FAR], T.bns[:, 0:FAR], T.bpn[:, 0:4 * FAR]).then_inc(sem.vbqn, 1)
+    ch("vi", v.tensor_scalar(T.lt[:, :], T.pl[:, :], 0, None, AluOpType.is_lt))
+    ch("vi", v.tensor_scalar(T.p2[:, :], T.pl[:, :], 4, None, AluOpType.arith_shift_right))
+    own("vz")
+    v.quantize_mx(T.bfq[:, FAR:2 * FAR], T.bfs[:, FAR:2 * FAR], T.bpf[:, 4 * FAR:8 * FAR]).then_inc(sem.vbo, 1)
+    own("vi")
+    ch("vi", v.tensor_scalar(T.p3[:, 0:3], T.p1[:, 0:3], 12, None, mult))
+    ch("vi", v.tensor_scalar(T.p3[:, 3:6], T.p1[:, 3:6], 12, 6, mult, add))
+    ch("vi", v.tensor_tensor(T.tm[:, :], T.lt[:, :], T.tr[:, :], mult))
+
+    def constant(t):
+        v.quantize_mx(T.kq[:, 128 * t:128 * t + 128], T.ks[:, 128 * t:128 * t + 128],
+                      T.cst[:, 3 - t:515 - t]).then_inc(sem.veq, 1)
+
+    v.wait_ge(sem.gcst, 1)
+    constant(0)
+    own("vi")
+    ch("vi", v.tensor_tensor(T.p4[:, :], T.p2[:, :], T.p3[:, :], add))
+    constant(1)
+    own("vi")
+    ch("vi", v.tensor_tensor(T.p5[:, :], T.p4[:, :], T.tm[:, :], add))
+    constant(2)
+    own("vi")
+    ch("vi", v.tensor_copy(T.po[:, :], T.p5[:, :]))
+    constant(3)
     te.wait_ge(sem.vbqn, 1)
     te.wait_ge(sem.acf, 3)
     te.wait_ge(sem.vf, 1)
     for i in range(4):
-        product("pa", i, "bnq", "bns", 0, FAR, True, True).then_inc(sem["tfn%d" % i], 1)
+        product("pa", i, "bnq", "bns", 0, True).then_inc(sem["tfn%d" % i], 1)
+    te.wait_ge(sem.vbo, 1)
     for i in range(4):
-        if i % 2 == 0:
-            s.wait_ge(sem["tfn%d" % i], 1)
-            s.activation(T.hn[:, i:4 * FAR:4], T["pa%d" % i][:, 0:FAR], copy).then_inc(sem.acfn, 1)
-        else:
-            v.wait_ge(sem["tfn%d" % i], 1)
-            v.tensor_copy(T.hn[:, i:4 * FAR:4], T["pa%d" % i][:, 0:FAR]).then_inc(sem.vfn, 1)
-    v.wait_ge(sem.acfn, 2)
-    v.wait_ge(sem.vfn, 2)
+        product("pb", i, "bfq", "bfs", FAR, False)
+    for i in range(4):
+        s.wait_ge(sem["tfn%d" % i], 1)
+        s.activation(T.hn[:, i:4 * FAR:4], T["pa%d" % i][:, 0:FAR], copy).then_inc(sem.acfn, 1)
+    v.wait_ge(sem.acfn, 4)
     v.quantize_mx(T.hnq[:, :], T.hns[:, :], T.hn[:, :]).then_inc(sem.vhn, 1)
+    v.quantize_mx(T.bnq[:, FAR:2 * FAR], T.bns[:, FAR:2 * FAR], T.bpn[:, 4 * FAR:8 * FAR]).then_inc(sem.vbno, 1)
     g.wait_ge(sem.vhn, 1)
     spread("hnq", "hns", LAND + 3 * UN, "arrn")
+    v.wait_ge(sem.gv, 2)
+    v.wait_ge(sem.gr, 1)
+    own("vi")
+    ch("vi", v.tensor_copy(T.inv[:, 0:288].indirect(T.po[:, 0:6]), T.val[:, :]))
+    ch("vi", v.tensor_scalar(T.m16[:, :], T.rv[:, :], T.pf[:, 0:1], None, AluOpType.is_equal))
+    own("vi")
+    ch("vi", v.tensor_tensor(T.f0[:, :], T.inv[:, 0:192], T.m16[:, :], mult))
+    own("vi")
+    ch("vi", v.tensor_tensor(T.f1[:, :], T.f0[:, 0:96], T.f0[:, 96:192], add))
+
+    def gather_sum(bank, tsem, asem, mid, part, out, done):
+        def last(t):
+            own("vx%d" % t)
+            v.tensor_tensor(out(t), T[bank + str(t)][:, 2 * UN:FAR], T[part][:, UN * t:UN * t + UN], add).then_inc(done(t), 1)
+
+        for t in range(4):
+            s.wait_ge(sem[tsem + str(t)], 1)
+            s.activation(T[mid][:, UN * t:UN * t + UN], T[bank + str(t)][:, UN:2 * UN], copy).then_inc(sem[asem + str(t)], 1)
+        for t in range(4):
+            v.wait_ge(sem[asem + str(t)], 1)
+            ch("vx%d" % t, v.tensor_tensor(T[part][:, UN * t:UN * t + UN], T[bank + str(t)][:, 0:UN],
+                                           T[mid][:, UN * t:UN * t + UN], add))
+            if t:
+                last(t - 1)
+        last(3)
 
     te.wait_ge(sem.veq, 4)
     for k in range(3):
         te.wait_ge(sem["arrf%d" % k], CODE_ENG[k][1] + PLANE_ENG[k][1])
-        for t in range(4):
-            m = unpack("pb", t, LAND + UN * (k + 1), False, k == 2)
-            if k == 2:
-                m.then_inc(sem["tg%d" % t], 1)
     for t in range(4):
-        if t % 2 == 0:
-            s.wait_ge(sem["tg%d" % t], 1)
-            s.activation(T.hg[:, 320 + t:512:4], T["pb%d" % t][:, 80:128], copy).then_inc(sem.acgg, 1)
-        else:
-            v.wait_ge(sem["tg%d" % t], 1)
-            v.tensor_copy(T.hg[:, 320 + t:512:4], T["pb%d" % t][:, 80:128]).then_inc(sem.vg, 1)
-    v.wait_ge(sem.acgg, 2)
-    v.wait_ge(sem.vg, 2)
+        unpack("pb", t, LAND, FAR, False).then_inc(sem["tg%d" % t], 1)
+    gather_sum("pb", "tg", "ag", "mg", "xg", lambda t: T.hg[:, 320 + t:512:4], lambda t: sem.vg)
+    v.wait_ge(sem.gh, 1)
+    v.wait_ge(sem.vg, 4)
     v.quantize_mx(T.hgq[:, :], T.hgs[:, :], T.hg[:, :]).then_inc(sem.vhg, 1)
     rid, pid = topo.addr(partner, core)
     m8 = emask(topo, core, partner, 0, 8)
@@ -248,75 +292,48 @@ def rank_program(g, core, T, topo):
     g.remote_dma(T.kq[:, at:at + UN].bitcast(dt.uint8), T.hgq[:, 80:128].bitcast(dt.uint8), sem.arrm, sem.lsend, pid, rid, m8)
     g.remote_dma(T.ks[:, at:at + UN], T.hgs[:, 80:128], sem.arrm, sem.lsend, pid, rid, m8)
 
-    te.wait_ge(sem.acfn, 2)
-    te.wait_ge(sem.vfn, 2)
+    own("vi")
+    ch("vi", v.tensor_tensor(T.f2[:, :], T.f1[:, 0:48], T.f1[:, 48:96], add))
+    ch("vz", v.memset(T.sn[:, :], 0.0))
+    own("vi")
+    ch("vi", v.tensor_tensor(T.f3[:, :], T.f2[:, 0:24], T.f2[:, 24:48], add))
+    ch("vz", v.memset(T.sf[:, :], 0.0))
+    own("vi")
+    ch("vi", v.tensor_tensor(T.f4[:, :], T.f3[:, 0:12], T.f3[:, 12:24], add))
+    own("vz")
+    own("vi")
+    v.tensor_copy(T.offi[:, :], T.f4[:, :]).then_inc(sem.vinv, 1)
+
+    te.wait_ge(sem.acfn, 4)
+    te.wait_ge(sem.vbno, 1)
     for i in range(4):
-        product("pa", i, "bnq", "bns", OWN0, H * UN, True, False)
+        product("pa", i, "bnq", "bns", FAR, False)
     for k in range(3):
         te.wait_ge(sem["arrn%d" % k], CODE_ENG[k][1] + PLANE_ENG[k][1])
-        for t in range(4):
-            m = unpack("pa", t, LAND + UN * (4 + k), False, k == 2)
-            if k == 2:
-                m.then_inc(sem["tn%d" % t], 1)
     for t in range(4):
-        s.wait_ge(sem["tn%d" % t], 1)
-        s.activation(T.sn[:, t:192:4], T["pa%d" % t][:, 80:128], copy).then_inc(sem.acnn, 1)
-
-    v.wait_ge(sem.pld, 128)
-    ch(v.tensor_scalar(T.lt[:, :], T.pl[:, :], 0, None, AluOpType.is_lt))
-    ch(v.tensor_scalar(T.tr[:, 0:3], T.ent[:, 0:3], 2 * OC + 1, None, add))
-    ch(v.tensor_scalar(T.tr[:, 3:6], T.ent[:, 3:6], OC + 1, None, add))
-    ch(v.tensor_scalar(T.p2[:, 0:3], T.pl[:, 0:3], 0, None, add))
-    ch(v.tensor_scalar(T.p2[:, 3:6], T.pl[:, 3:6], OC, None, add))
-    ch(v.tensor_scalar(T.rq[:, :], T.ipm[:, 0:2], 2, 3, AluOpType.arith_shift_right, AluOpType.bitwise_and))
-    ch(v.tensor_scalar(T.tq[:, :], T.ipm[:, 0:2], 3, None, AluOpType.bitwise_and))
-    own()
-    ch(v.tensor_tensor(T.tm[:, :], T.lt[:, :], T.tr[:, :], mult))
-    for r in range(4):
-        ch(v.tensor_scalar(T.mk[:, r:r + 1], T.rq[:, 0:1], r, 4, AluOpType.is_equal, mult))
-    ch(v.tensor_copy(T.tc[:, :], T.tq[:, :]))
-    own()
-    ch(v.tensor_tensor(T.p3[:, :], T.p2[:, :], T.tm[:, :], add))
-    own()
-    ch(v.tensor_copy(T.po[:, :], T.p3[:, :]))
-    v.wait_ge(sem.gv, 1)
-    own()
-    ch(v.tensor_copy(T.inv[:, 0:272].indirect(T.po[:, 0:6]), T.val[:, :]))
-    own()
-    ch(v.tensor_scalar(T.s0[:, :], T.inv[:, 0:176:4], T.mk[:, 0:1], T.tc[:, 0:1], mult, add))
-    for r in range(1, 4):
-        ch(v.tensor_scalar(T["s%d" % r][:, :], T.inv[:, r:176:4], T.mk[:, r:r + 1], None, mult))
-    own()
-    ch(v.tensor_tensor(T.s0[:, :], T.s0[:, :], T.s1[:, :], add))
-    ch(v.tensor_tensor(T.s2[:, :], T.s2[:, :], T.s3[:, :], add))
-    own()
-    ch(v.tensor_tensor(T.s0[:, :], T.s0[:, :], T.s2[:, :], add))
-    own()
-    v.tensor_copy(T.offi[:, :], T.s0[:, :]).then_inc(sem.vinv, 1)
-    gn, gf = 22 * topo.host(core), 22 * topo.host(partner)
+        unpack("pa", t, LAND + FAR, FAR, False).then_inc(sem["tn%d" % t], 1)
+    gather_sum("pa", "tn", "an", "mn", "xn", lambda t: T.sn[:, WIN * t:WIN * t + UN], lambda t: sem["vn%d" % t])
+    gn, gf = 6 * topo.host(core), 6 * topo.host(partner)
     s.wait_ge(sem.vinv, 1)
-    s.wait_ge(sem.acnn, 4)
-    s.activation(T.yn[:, :], T.sn[:, 0:200].indirect(T.offi[:, gn:gn + 22]), copy).then_inc(sem.ayn, 1)
+    for t in range(4):
+        s.wait_ge(sem["vn%d" % t], 1)
+        s.activation(T.yn[:, OP * t:OP * t + OP], T.sn[:, WIN * t:WIN * t + WIN].indirect(T.offi[:, gn:gn + 6]),
+                     copy).then_inc(sem.ayn, 1)
 
     te.wait_ge(sem.arrm, 16)
-    te.wait_ge(sem.acgg, 2)
-    te.wait_ge(sem.vg, 2)
+    te.wait_ge(sem.vg, 4)
     for t in range(4):
-        unpack("pb", t, at + UN, True, True).then_inc(sem["tl%d" % t], 1)
+        unpack("pb", t, at + UN - 128, 128, True).then_inc(sem["tl%d" % t], 1)
     for t in range(4):
-        if t % 2 == 0:
-            s.wait_ge(sem["tl%d" % t], 1)
-            s.activation(T.sf[:, t:192:4], T["pb%d" % t][:, 80:128], copy).then_inc(sem.acm, 1)
-        else:
-            v.wait_ge(sem["tl%d" % t], 1)
-            v.tensor_copy(T.sf[:, t:192:4], T["pb%d" % t][:, 80:128]).then_inc(sem.vm, 1)
-    own()
+        s.wait_ge(sem["tl%d" % t], 1)
+        s.activation(T.sf[:, WIN * t:WIN * t + UN], T["pb%d" % t][:, 80:128], copy).then_inc(sem["am%d" % t], 1)
     v.wait_ge(sem.vinv, 1)
-    v.wait_ge(sem.ayn, 1)
-    v.wait_ge(sem.acm, 2)
-    v.wait_ge(sem.vm, 2)
-    v.tensor_tensor(T.yo[:, :], T.sf[:, 0:200].indirect(T.offi[:, gf:gf + 22]), T.yn[:, :], add).then_inc(sem.vy, 1)
-    sy.wait_ge(sem.vy, 1)
-    sy.dma_start(T.y[:, :], T.yo[:, :]).then_inc(sem.yst, 16)
+    v.wait_ge(sem.ayn, 4)
+    for t in range(4):
+        v.wait_ge(sem["am%d" % t], 1)
+        v.tensor_tensor(T.yo[:, t:4 * OP:4], T.sf[:, WIN * t:WIN * t + WIN].indirect(T.offi[:, gf:gf + 6]),
+                        T.yn[:, OP * t:OP * t + OP], add).then_inc(sem.vy, 1)
+    sy.wait_ge(sem.vy, 4)
+    sy.dma_start(T.y[:, :], T.yo[:, 0:4 * OC]).then_inc(sem.yst, 16)
     sy.wait_ge(sem.yst, 16)
     g.wait_ge(sem.lsend, 48)

from concourse.bass import DstId, RemoteDMATransfer
from concourse.mybir import dt, AluOpType, ActivationFunctionType

N, TCOL, CAPP, OC, UN = 8, 192, 24, 88, 48
H = 4
FAR = (H - 1) * UN
LAND = 512
OP = 96
WIN = 56

F32, BF, I32, U16 = "float32", "bfloat16", "int32", "uint16"
CODE, PLANE = "float8_e4m3fn_x4", "uint8"
SCRATCH = {
    "asb": ("sbuf", [128, 2048], BF), "bsb": ("sbuf", [128, 4 * TCOL], BF),
    "sl": ("sbuf", [128, 12], I32), "ul": ("sbuf", [128, 12], I32), "pl": ("sbuf", [128, 6], I32),
    "ones": ("sbuf", [128, 516], BF), "cst": ("sbuf", [128, 516], BF),
    "ipm": ("sbuf", [128, 12], I32), "ek": ("sbuf", [128, 12], I32), "q15": ("sbuf", [128, 12], I32),
    "ent": ("sbuf", [128, 12], I32), "w1": ("sbuf", [128, 12], I32), "w2": ("sbuf", [128, 12], I32),
    "dsl": ("sbuf", [128, 12], I32), "x2": ("sbuf", [128, 12], I32),
    "offs": ("sbuf", [128, 48], U16), "offu": ("sbuf", [128, 48], U16),
    "bgf": ("sbuf", [128, 384], BF), "bgn": ("sbuf", [128, 384], BF),
    "bpf": ("sbuf", [128, 8 * FAR], BF), "bpn": ("sbuf", [128, 8 * FAR], BF),
    "aq": ("sbuf", [128, 512], CODE), "asc": ("sbuf", [128, 512], PLANE),
    "bfq": ("sbuf", [128, 2 * FAR], CODE), "bfs": ("sbuf", [128, 2 * FAR], PLANE),
    "bnq": ("sbuf", [128, 2 * FAR], CODE), "bns": ("sbuf", [128, 2 * FAR], PLANE),
    "hf": ("sbuf", [128, 4 * FAR], BF), "hfq": ("sbuf", [128, FAR], CODE), "hfs": ("sbuf", [128, FAR], PLANE),
    "hn": ("sbuf", [128, 4 * FAR], BF), "hnq": ("sbuf", [128, FAR], CODE), "hns": ("sbuf", [128, FAR], PLANE),
    "hg": ("sbuf", [128, 512], BF), "hgq": ("sbuf", [128, 128], CODE), "hgs": ("sbuf", [128, 128], PLANE),
    "kq": ("sbuf", [128, LAND + 7 * UN], CODE), "ks": ("sbuf", [128, LAND + 7 * UN], PLANE),
    "mg": ("sbuf", [128, 4 * UN], F32), "xg": ("sbuf", [128, 4 * UN], F32),
    "mn": ("sbuf", [128, 4 * UN], F32), "xn": ("sbuf", [128, 4 * UN], F32),
    "val": ("sbuf", [128, 96], F32), "inv": ("sbuf", [128, 288], F32), "rv": ("sbuf", [128, 192], F32),
    "m16": ("sbuf", [128, 192], F32), "pf": ("sbuf", [128, 2], F32),
    "lt": ("sbuf", [128, 6], I32), "tr": ("sbuf", [128, 6], I32), "tm": ("sbuf", [128, 6], I32),
    "p1": ("sbuf", [128, 6], I32), "p2": ("sbuf", [128, 6], I32), "p3": ("sbuf", [128, 6], I32),
    "p4": ("sbuf", [128, 6], I32), "p5": ("sbuf", [128, 6], I32), "po": ("sbuf", [128, 6], U16),
    "f0": ("sbuf", [128, 192], F32), "f1": ("sbuf", [128, 96], F32), "f2": ("sbuf", [128, 48], F32),
    "f3": ("sbuf", [128, 24], F32), "f4": ("sbuf", [128, 12], F32), "offi": ("sbuf", [128, 12], U16),
    "sn": ("sbuf", [128, 4 * WIN], F32), "sf": ("sbuf", [128, 4 * WIN], F32),
    "yn": ("sbuf", [128, 4 * OP], F32), "yo": ("sbuf", [128, 4 * OP], F32),
}
for _i in range(4):
    SCRATCH["pa%d" % _i] = ("psum", [128, 512], F32)
    SCRATCH["pb%d" % _i] = ("psum", [128, 512], F32)

SEMAPHORES = (["sld", "uld", "pld", "bld", "ald0", "ald1", "yst", "lsend", "ones", "gi", "gcst", "gz", "gh", "gv", "gr", "vc",
               "vq", "vi", "vz", "veq", "voff", "voffn", "vbq", "vbqn", "vbo", "vbno", "vf", "vg", "vhf", "vhn",
               "vhg", "vinv", "vy", "acg", "acn", "acf", "acfn", "ayn", "arrm"]
              + [p + str(i) for p in ("vaq", "tf", "tfn", "tg", "tn", "tl", "ag", "an", "am", "vx", "vn") for i in range(4)]
              + ["arrf%d" % i for i in range(3)] + ["arrn%d" % i for i in range(3)])


def slot_of(topo, dst, src):
    if topo.mates(dst, src):
        return 0
    return 1 if topo.same_plane(dst, src) else 2


CODE_ENG = {0: (4, 2), 1: (6, 2), 2: (0, 4)}
PLANE_ENG = {0: (0, 2), 1: (2, 2), 2: (4, 4)}


def emask(topo, src, dst, first, count):
    return sum(1 << e for e in topo.engines(src, dst)[first:first + count])


def rank_program(g, core, T, topo):
    rank = T.rank_of(core)
    if rank is None:
        return
    v, s, te, sy, sem = g.vector, g.scalar, g.tensor, g.sync, T.sem
    add, mult = AluOpType.add, AluOpType.mult
    copy = ActivationFunctionType.Copy
    here = [r for r in range(N) if topo.host(T.cores[r]) == topo.host(core)]
    there = [r for r in range(N) if topo.host(T.cores[r]) != topo.host(core)]
    my = here.index(rank)
    f0, n0 = there[0] * CAPP // 16, here[0] * CAPP // 16
    peers = [T.cores[here[(my + 1 + j) % H]] for j in range(H - 1)]
    partner = T.cores[there[my]]

    cnt = {"vc": 0, "vq": 0, "vi": 0, "vz": 0, "vx0": 0, "vx1": 0, "vx2": 0, "vx3": 0}

    def ch(name, ins):
        ins.then_inc(sem[name], 1)
        cnt[name] += 1

    def own(name):
        v.wait_ge(sem[name], cnt[name])

    def fill(out, pattern, base, done):
        g.iota(out, pattern, base, 0, allow_small_or_imprecise_dtypes=True).then_inc(done, 1)

    for k in range(8):
        (sy if k < 4 else s).dma_start(T.sl[16 * k:16 * k + 16, :], T.send[:, :]).then_inc(sem.sld, 16)
    sy.dma_start(T.bsb[:, :], T.b[:, :]).then_inc(sem.bld, 16)
    for k in range(8):
        (sy if k < 3 else s).dma_start(T.ul[16 * k:16 * k + 16, :], T.un[:, :]).then_inc(sem.uld, 16)
    sy.dma_start(T.asb[:, 0:1536], T.a[:, 0:1536]).then_inc(sem.ald0, 16)
    sy.dma_start(T.asb[:, 1536:2048], T.a[:, 1536:2048]).then_inc(sem.ald1, 16)
    for k in range(8):
        sy.dma_start(T.pl[16 * k:16 * k + 16, :], T.upl[:, :]).then_inc(sem.pld, 16)

    g.iota(T.ipm[:, :], [[0, 12]], 0, 1).then_inc(sem.gi, 1)
    g.iota(T.ek[:, :], [[16, 12]], 0, 0).then_inc(sem.gi, 1)
    g.wait_ge(sem.ones, 1)
    g.affine_select(T.cst[:, :], T.ones[:, :], [[1, 516]], AluOpType.is_equal, 0.0, -3, -4).then_inc(sem.gcst, 1)
    fill(T.bpn[:, :], [[0, 8 * FAR]], 0, sem.gz)
    fill(T.rv[:, :], [[1, 16], [0, 12]], 0, sem.gr)

    v.memset(T.ones[:, :], 1.0).then_inc(sem.ones, 1)
    v.wait_ge(sem.gi, 2)
    ch("vc", v.tensor_scalar(T.q15[:, :], T.ipm[:, :], 15, None, AluOpType.bitwise_and))
    ch("vq", v.memset(T.bpf[:, 0:768], 0.0))
    own("vc")
    ch("vc", v.tensor_tensor(T.ent[:, :], T.q15[:, :], T.ek[:, :], add))
    ch("vi", v.tensor_copy(T.pf[:, :], T.q15[:, 0:2]))
    own("vc")
    ch("vc", v.tensor_scalar(T.w1[:, :], T.ent[:, :], 683, (3 - my) << 14, mult, add))
    ch("vi", v.tensor_scalar(T.tr[:, 0:3], T.ent[:, 0:3], 13, None, add))
    ch("vi", v.tensor_scalar(T.tr[:, 3:6], T.ent[:, 3:6], 7, None, add))
    own("vc")
    ch("vc", v.tensor_scalar(T.w2[:, :], T.w1[:, :], 14, 3, AluOpType.arith_shift_right, AluOpType.bitwise_and))
    own("vc")
    ch("vc", v.tensor_scalar(T.dsl[:, :], T.w2[:, :], UN, None, mult))

    v.wait_ge(sem.sld, 128)
    for t in range(4):
        v.tensor_scalar(T.offs[:, 6 * t:6 * t + 6], T.sl[:, f0:f0 + 6], 4, t, mult, add).then_inc(sem.voff, 1)
    v.wait_ge(sem.uld, 128)
    own("vc")
    ch("vc", v.tensor_tensor(T.x2[:, :], T.ul[:, :], T.dsl[:, :], add))
    for t in range(4):
        v.tensor_scalar(T.offs[:, 24 + 6 * t:30 + 6 * t], T.sl[:, n0:n0 + 6], 4, t, mult, add).then_inc(sem.voffn, 1)
    own("vc")
    for t in range(4):
        ch("vq", v.tensor_scalar(T.offu[:, 6 * t:6 * t + 6], T.x2[:, f0:f0 + 6], 4, t, mult, add))
    s.wait_ge(sem.bld, 16)
    s.wait_ge(sem.voff, 4)
    s.activation(T.bgf[:, :], T.bsb[:, 0:768].indirect(T.offs[:, 0:24]), copy).then_inc(sem.acg, 1)
    s.wait_ge(sem.voffn, 4)
    s.activation(T.bgn[:, :], T.bsb[:, 0:768].indirect(T.offs[:, 24:48]), copy).then_inc(sem.acn, 1)
    own("vq")
    v.wait_ge(sem.acg, 1)
    ch("vq", v.tensor_copy(T.bpf[:, 0:768].indirect(T.offu[:, 0:24]), T.bgf[:, :]))

    def quantise_a(i):
        v.quantize_mx(T.aq[:, 128 * i:128 * i + 128], T.asc[:, 128 * i:128 * i + 128],
                      T.asb[:, 512 * i:512 * i + 512]).then_inc(sem["vaq%d" % i], 1)

    v.wait_ge(sem.ald0, 16)
    quantise_a(0)
    own("vq")
    v.quantize_mx(T.bfq[:, 0:FAR], T.bfs[:, 0:FAR], T.bpf[:, 0:4 * FAR]).then_inc(sem.vbq, 1)
    quantise_a(1)
    quantise_a(2)
    v.wait_ge(sem.ald1, 16)
    quantise_a(3)
    for t in range(4):
        ch("vq", v.tensor_scalar(T.offu[:, 24 + 6 * t:30 + 6 * t], T.x2[:, n0:n0 + 6], 4, t, mult, add))

    def product(bank, i, q, p, c0, stop):
        return te.matmul_mx(T[bank + str(i)][:, 0:FAR], T.aq[:, 128 * i:128 * i + 128], T.asc[:, 128 * i:128 * i + 128],
                            T[q][:, c0:c0 + FAR], T[p][:, c0:c0 + FAR], True, stop)

    def unpack(bank, t, c0, n, start):
        return te.matmul_mx(T[bank + str(t)][:, 0:n], T.kq[:, 128 * t:128 * t + 128], T.ks[:, 128 * t:128 * t + 128],
                            T.kq[:, c0:c0 + n], T.ks[:, c0:c0 + n], start, True)

    te.wait_ge(sem.vbq, 1)
    for i in range(4):
        te.wait_ge(sem["vaq%d" % i], 1)
        product("pa", i, "bfq", "bfs", 0, True).then_inc(sem["tf%d" % i], 1)
    for i in range(3):
        s.wait_ge(sem["tf%d" % i], 1)
        s.activation(T.hf[:, i:4 * FAR:4], T["pa%d" % i][:, 0:FAR], copy).then_inc(sem.acf, 1)
    v.wait_ge(sem.tf3, 1)
    v.tensor_copy(T.hf[:, 3:4 * FAR:4], T.pa3[:, 0:FAR]).then_inc(sem.vf, 1)
    v.wait_ge(sem.acf, 3)
    v.wait_ge(sem.vf, 1)
    v.quantize_mx(T.hfq[:, :], T.hfs[:, :], T.hf[:, :]).then_inc(sem.vhf, 1)

    def spread(q, p, at, name):
        codes, planes = [], []
        for j, d in enumerate(peers):
            k = slot_of(topo, d, core)
            rid, pid = topo.addr(d, core)
            a, b = at + UN * k, at + UN * (k + 1)
            codes.append(RemoteDMATransfer(
                dst_ids=[DstId(rid=rid, pnc=pid)], dma_engine_mask=emask(topo, core, d, *CODE_ENG[k]),
                remote_sem=sem[name + str(k)], src=T[q][:, UN * j:UN * j + UN].bitcast(dt.uint8),
                dst=T.kq[:, a:b].bitcast(dt.uint8)))
            planes.append(RemoteDMATransfer(
                dst_ids=[DstId(rid=rid, pnc=pid)], dma_engine_mask=emask(topo, core, d, *PLANE_ENG[k]),
                remote_sem=sem[name + str(k)], src=T[p][:, UN * j:UN * j + UN], dst=T.ks[:, a:b]))
        g.remote_dma_fused(codes, local_sem=sem.lsend)
        g.remote_dma_fused(planes, local_sem=sem.lsend)

    g.wait_ge(sem.vhf, 1)
    spread("hfq", "hfs", LAND, "arrf")
    fill(T.inv[:, :], [[0, 288]], UN, sem.gv)
    fill(T.val[:, :], [[0, 2], [1, 48]], 0, sem.gv)
    fill(T.hg[:, 0:320], [[0, 320]], 0, sem.gh)

    v.wait_ge(sem.acn, 1)
    v.wait_ge(sem.gz, 1)
    own("vq")
    ch("vq", v.tensor_copy(T.bpn[:, 0:768].indirect(T.offu[:, 24:48]), T.bgn[:, :]))
    ch("vz", v.memset(T.bpf[:, 768:8 * FAR], 0.0))
    v.wait_ge(sem.pld, 128)
    ch("vi", v.tensor_scalar(T.p1[:, :], T.pl[:, :], 15, None, AluOpType.bitwise_and))
    own("vq")
    v.quantize_mx(T.bnq[:, 0:FAR], T.bns[:, 0:FAR], T.bpn[:, 0:4 * FAR]).then_inc(sem.vbqn, 1)
    ch("vi", v.tensor_scalar(T.lt[:, :], T.pl[:, :], 0, None, AluOpType.is_lt))
    ch("vi", v.tensor_scalar(T.p2[:, :], T.pl[:, :], 4, None, AluOpType.arith_shift_right))
    own("vz")
    v.quantize_mx(T.bfq[:, FAR:2 * FAR], T.bfs[:, FAR:2 * FAR], T.bpf[:, 4 * FAR:8 * FAR]).then_inc(sem.vbo, 1)
    own("vi")
    ch("vi", v.tensor_scalar(T.p3[:, 0:3], T.p1[:, 0:3], 12, None, mult))
    ch("vi", v.tensor_scalar(T.p3[:, 3:6], T.p1[:, 3:6], 12, 6, mult, add))
    ch("vi", v.tensor_tensor(T.tm[:, :], T.lt[:, :], T.tr[:, :], mult))

    def constant(t):
        v.quantize_mx(T.kq[:, 128 * t:128 * t + 128], T.ks[:, 128 * t:128 * t + 128],
                      T.cst[:, 3 - t:515 - t]).then_inc(sem.veq, 1)

    v.wait_ge(sem.gcst, 1)
    constant(0)
    own("vi")
    ch("vi", v.tensor_tensor(T.p4[:, :], T.p2[:, :], T.p3[:, :], add))
    constant(1)
    own("vi")
    ch("vi", v.tensor_tensor(T.p5[:, :], T.p4[:, :], T.tm[:, :], add))
    constant(2)
    own("vi")
    ch("vi", v.tensor_copy(T.po[:, :], T.p5[:, :]))
    constant(3)
    te.wait_ge(sem.vbqn, 1)
    te.wait_ge(sem.acf, 3)
    te.wait_ge(sem.vf, 1)
    for i in range(4):
        product("pa", i, "bnq", "bns", 0, True).then_inc(sem["tfn%d" % i], 1)
    te.wait_ge(sem.vbo, 1)
    for i in range(4):
        product("pb", i, "bfq", "bfs", FAR, False)
    for i in range(4):
        s.wait_ge(sem["tfn%d" % i], 1)
        s.activation(T.hn[:, i:4 * FAR:4], T["pa%d" % i][:, 0:FAR], copy).then_inc(sem.acfn, 1)
    v.wait_ge(sem.acfn, 4)
    v.quantize_mx(T.hnq[:, :], T.hns[:, :], T.hn[:, :]).then_inc(sem.vhn, 1)
    v.quantize_mx(T.bnq[:, FAR:2 * FAR], T.bns[:, FAR:2 * FAR], T.bpn[:, 4 * FAR:8 * FAR]).then_inc(sem.vbno, 1)
    g.wait_ge(sem.vhn, 1)
    spread("hnq", "hns", LAND + 3 * UN, "arrn")
    v.wait_ge(sem.gv, 2)
    v.wait_ge(sem.gr, 1)
    own("vi")
    ch("vi", v.tensor_copy(T.inv[:, 0:288].indirect(T.po[:, 0:6]), T.val[:, :]))
    ch("vi", v.tensor_scalar(T.m16[:, :], T.rv[:, :], T.pf[:, 0:1], None, AluOpType.is_equal))
    own("vi")
    ch("vi", v.tensor_tensor(T.f0[:, :], T.inv[:, 0:192], T.m16[:, :], mult))
    own("vi")
    ch("vi", v.tensor_tensor(T.f1[:, :], T.f0[:, 0:96], T.f0[:, 96:192], add))

    def gather_sum(bank, tsem, asem, mid, part, out, done):
        def last(t):
            own("vx%d" % t)
            v.tensor_tensor(out(t), T[bank + str(t)][:, 2 * UN:FAR], T[part][:, UN * t:UN * t + UN], add).then_inc(done(t), 1)

        for t in range(4):
            s.wait_ge(sem[tsem + str(t)], 1)
            s.activation(T[mid][:, UN * t:UN * t + UN], T[bank + str(t)][:, UN:2 * UN], copy).then_inc(sem[asem + str(t)], 1)
        for t in range(4):
            v.wait_ge(sem[asem + str(t)], 1)
            ch("vx%d" % t, v.tensor_tensor(T[part][:, UN * t:UN * t + UN], T[bank + str(t)][:, 0:UN],
                                           T[mid][:, UN * t:UN * t + UN], add))
            if t:
                last(t - 1)
        last(3)

    te.wait_ge(sem.veq, 4)
    for k in range(3):
        te.wait_ge(sem["arrf%d" % k], CODE_ENG[k][1] + PLANE_ENG[k][1])
    for t in range(4):
        unpack("pb", t, LAND, FAR, False).then_inc(sem["tg%d" % t], 1)
    gather_sum("pb", "tg", "ag", "mg", "xg", lambda t: T.hg[:, 320 + t:512:4], lambda t: sem.vg)
    v.wait_ge(sem.gh, 1)
    v.wait_ge(sem.vg, 4)
    v.quantize_mx(T.hgq[:, :], T.hgs[:, :], T.hg[:, :]).then_inc(sem.vhg, 1)
    rid, pid = topo.addr(partner, core)
    m8 = emask(topo, core, partner, 0, 8)
    at = LAND + 6 * UN
    g.wait_ge(sem.vhg, 1)
    g.remote_dma(T.kq[:, at:at + UN].bitcast(dt.uint8), T.hgq[:, 80:128].bitcast(dt.uint8), sem.arrm, sem.lsend, pid, rid, m8)
    g.remote_dma(T.ks[:, at:at + UN], T.hgs[:, 80:128], sem.arrm, sem.lsend, pid, rid, m8)

    own("vi")
    ch("vi", v.tensor_tensor(T.f2[:, :], T.f1[:, 0:48], T.f1[:, 48:96], add))
    ch("vz", v.memset(T.sn[:, :], 0.0))
    own("vi")
    ch("vi", v.tensor_tensor(T.f3[:, :], T.f2[:, 0:24], T.f2[:, 24:48], add))
    ch("vz", v.memset(T.sf[:, :], 0.0))
    own("vi")
    ch("vi", v.tensor_tensor(T.f4[:, :], T.f3[:, 0:12], T.f3[:, 12:24], add))
    own("vz")
    own("vi")
    v.tensor_copy(T.offi[:, :], T.f4[:, :]).then_inc(sem.vinv, 1)

    te.wait_ge(sem.acfn, 4)
    te.wait_ge(sem.vbno, 1)
    for i in range(4):
        product("pa", i, "bnq", "bns", FAR, False)
    for k in range(3):
        te.wait_ge(sem["arrn%d" % k], CODE_ENG[k][1] + PLANE_ENG[k][1])
    for t in range(4):
        unpack("pa", t, LAND + FAR, FAR, False).then_inc(sem["tn%d" % t], 1)
    gather_sum("pa", "tn", "an", "mn", "xn", lambda t: T.sn[:, WIN * t:WIN * t + UN], lambda t: sem["vn%d" % t])
    gn, gf = 6 * topo.host(core), 6 * topo.host(partner)
    s.wait_ge(sem.vinv, 1)
    for t in range(4):
        s.wait_ge(sem["vn%d" % t], 1)
        s.activation(T.yn[:, OP * t:OP * t + OP], T.sn[:, WIN * t:WIN * t + WIN].indirect(T.offi[:, gn:gn + 6]),
                     copy).then_inc(sem.ayn, 1)

    te.wait_ge(sem.arrm, 16)
    te.wait_ge(sem.vg, 4)
    for t in range(4):
        unpack("pb", t, at + UN - 128, 128, True).then_inc(sem["tl%d" % t], 1)
    for t in range(4):
        s.wait_ge(sem["tl%d" % t], 1)
        s.activation(T.sf[:, WIN * t:WIN * t + UN], T["pb%d" % t][:, 80:128], copy).then_inc(sem["am%d" % t], 1)
    v.wait_ge(sem.vinv, 1)
    v.wait_ge(sem.ayn, 4)
    for t in range(4):
        v.wait_ge(sem["am%d" % t], 1)
        v.tensor_tensor(T.yo[:, t:4 * OP:4], T.sf[:, WIN * t:WIN * t + WIN].indirect(T.offi[:, gf:gf + 6]),
                        T.yn[:, OP * t:OP * t + OP], add).then_inc(sem.vy, 1)
    sy.wait_ge(sem.vy, 4)
    sy.dma_start(T.y[:, :], T.yo[:, 0:4 * OC]).then_inc(sem.yst, 16)
    sy.wait_ge(sem.yst, 16)
    g.wait_ge(sem.lsend, 48)
